import numpy as np
import ml_dtypes


def mxq(x, axis, fmt="e4m3"):
    dtype, down = {"e4m3": (ml_dtypes.float8_e4m3fn, 7), "e5m2": (ml_dtypes.float8_e5m2, 14)}[fmt]
    v = np.moveaxis(np.asarray(x, np.float32).astype(ml_dtypes.bfloat16).astype(np.float64), axis, -1)
    blocks = v.reshape(v.shape[:-1] + (-1, 32))
    amax = np.abs(blocks).max(-1, keepdims=True)
    byte = np.maximum(np.where(amax > 0, np.frexp(amax)[1] - 1 + 127, 0) - down, 1)
    scale = np.exp2(byte - 127.0)
    codes = (blocks / scale).astype(np.float32).astype(dtype).astype(np.float64)
    return np.moveaxis((codes * scale).reshape(v.shape), -1, axis)


WIDE = False


def mx_kscale(k):
    if not WIDE:
        return np.ones(k)
    levels = np.array([10, -10, 5, -5, 0])
    if k % 512:
        return np.exp2(np.random.permutation(np.resize(levels, k // 32))).repeat(32)
    a = np.empty((k // 512, 16))
    for p in range(k // 512):
        a[p, :8] = np.random.permutation(np.resize(levels, 8))
        for g in range(8):
            far = levels[np.abs(levels - a[p, g]) >= 10]
            a[p, g + 8] = far[np.random.randint(len(far))]
    return np.exp2(a.ravel()).repeat(32)


def f64(x):
    return np.asarray(x).astype(np.float64)


def striped(idx):
    return np.tile(idx.reshape(-1, 16).T, (8, 1)).astype(np.uint16)


def unstriped(offs):
    return offs[:16].T.reshape(-1).astype(np.int64)


E2M1 = np.array([0.0, 0.5, 1.0, 1.5, 2.0, 3.0, 4.0, 6.0, -0.0, -0.5, -1.0, -1.5, -2.0, -3.0, -4.0, -6.0])


def pack_weight(w, fmt):
    k, n = w.shape
    w = f64(np.asarray(w, np.float32).astype(ml_dtypes.bfloat16)).reshape(k // 32, 32, n)
    amax = np.abs(w).max(1)
    if fmt == "e4m3":
        byte = np.frexp(amax)[1] - 1 + 127 - 7
    else:
        mant, ex = np.frexp(amax / 6.0)
        byte = np.where(mant > 0.5, ex, ex - 1) + 127
    byte = np.clip(np.where(amax > 0, byte, 1), 1, 254)
    scaled = (w * np.exp2(127.0 - byte)[:, None, :]).reshape(k, n).astype(np.float32)
    by_word = np.ascontiguousarray(scaled.reshape(k // 512, 128, 4, n).transpose(0, 1, 3, 2))
    if fmt == "e4m3":
        words = by_word.astype(ml_dtypes.float8_e4m3fn).view(np.uint8)
    else:
        c = by_word.astype(ml_dtypes.float4_e2m1fn).view(np.uint8) & 0xF
        words = (c[..., 0::2] | (c[..., 1::2] << 4)).reshape(k // 512, 128, 2 * n)
    return np.ascontiguousarray(words), np.ascontiguousarray(byte.astype(np.uint8).reshape(k // 512, 16, n))


def unpack_weight(words, scales, fmt):
    g, _, n = scales.shape
    words = np.ascontiguousarray(words).reshape(g, 128, n, -1)
    if fmt == "e4m3":
        vals = words.view(ml_dtypes.float8_e4m3fn).astype(np.float64)
    else:
        nib = np.empty((g, 128, n, 4), np.uint8)
        nib[..., 0::2] = words & 0xF
        nib[..., 1::2] = words >> 4
        vals = E2M1[nib]
    vals = vals * np.repeat(np.exp2(scales.astype(np.float64) - 127.0), 8, axis=1)[..., None]
    return vals.transpose(0, 1, 3, 2).reshape(g * 512, n)


def gelu(v):
    return 0.5 * v * (1.0 + np.tanh(np.sqrt(2.0 / np.pi) * (v + 0.044715 * v**3)))


def striped8(idx):
    return np.concatenate([v.reshape(-1, 16).T for v in idx]).astype(np.uint16)


def unstriped8(offs):
    return np.stack([offs[16 * g:16 * g + 16].T.reshape(-1) for g in range(8)]).astype(np.int64)


def runs(v, idx8):
    k = np.arange(v.shape[0])
    return v[k[:, None], idx8[k % 512 // 64]]


def bf(x):
    return np.asarray(x, np.float32).astype(ml_dtypes.bfloat16)


def planes(Y):
    n, m = Y.shape
    b = f64(bf(Y)).reshape(n // 32, 32, m)
    amax = np.abs(b).max(1)
    byte = np.clip(np.where(amax > 0, np.frexp(amax)[1] - 1 + 127 - 7, 1), 1, 254)
    codes = (b * np.exp2(127.0 - byte)[:, None, :]).reshape(n, m).astype(np.float32).astype(ml_dtypes.float8_e4m3fn).view(np.uint8)
    words = codes.reshape(n // 512, 128, 4, m).transpose(0, 1, 3, 2)
    return np.ascontiguousarray(words), np.ascontiguousarray(byte.astype(np.uint8).reshape(n // 512, 16, m))


K, T, S, H, P, N, G = 1536, 2048, 1024, 1024, 512, 512, 8

def setup_inputs():
    n = np.random.standard_normal
    s = mx_kscale(K)[:, None]
    u = mx_kscale(H)[:, None]
    tab_words, tab_scales = pack_weight(n((K, T)) * s, "e4m3")
    w1_words, w1_scales = pack_weight(0.75 * n((K, H)) / np.sqrt(K) / s, "e2m1")
    sign = np.where(n(H) > 0, 1.0, -1.0)
    gain = sign * np.random.uniform(2.0, 5.0, H) * u[:, 0]
    w2 = n((H, N)) / np.sqrt(H) / u * np.exp(0.8 * n(N))[None, :]
    idx8 = np.stack([np.random.permutation(S)[:P] for _ in range(G)])
    return {
        "tab_words": tab_words, "tab_scales": tab_scales,
        "offs": striped(np.random.permutation(T)[:S]),
        "offs2": striped8(idx8),
        "w1_words": w1_words, "w1_scales": w1_scales,
        "gain": gain.astype(np.float32),
        "w2": w2.astype(np.float32),
    }

def reference(tab_words, tab_scales, offs, offs2, w1_words, w1_scales, gain, w2):
    v = unpack_weight(tab_words, tab_scales, "e4m3")[:, unstriped(offs)]
    w1 = unpack_weight(w1_words, w1_scales, "e2m1")
    h = w1.T @ v
    top = h.max(axis=1)
    hp = runs(h, unstriped8(offs2))
    a = np.exp(hp - top[:, None])
    b = f64(gain)[:, None] * a
    y = mxq(f64(w2), 0, "e4m3").T @ mxq(b, 0, "e4m3")
    words, scales = planes(y)
    return y, words, scales

@@ -1,0 +1,274 @@
+from contextlib import ExitStack
+
+import concourse.mybir as mybir
+
+K, T, S, H, M, N = 1536, 2048, 1024, 1024, 512, 512
+FLOPS = 2 * K * H * S + 2 * H * N * M
+
+F32 = mybir.dt.float32
+BF16 = mybir.dt.bfloat16
+I32 = mybir.dt.int32
+U32 = mybir.dt.uint32
+U16 = mybir.dt.uint16
+U8 = mybir.dt.uint8
+E4M3 = mybir.dt.float8_e4m3fn_x4
+E2M1 = mybir.dt.float4_e2m1fn_x4
+ALU = mybir.AluOpType
+ACT = mybir.ActivationFunctionType
+
+P = 128
+PACK = 4
+PASSES = K // (P * PACK)
+GROUPS = H // (P * PACK)
+BANK = 512
+HALVES = S // BANK
+QUADS = 4
+MQ = 128
+
+
+def tile_list_talker_locator_kernel(
+    tc, tab_words, tab_scales, offs, offs2, w1_words, w1_scales, gain, w2, out_0, out_1, out_2
+):
+    nc = tc.nc
+    with ExitStack() as ctx:
+        keep = ctx.enter_context(tc.tile_pool(name="keep", bufs=1))
+        psum = ctx.enter_context(tc.psum_pool(name="psum", bufs=8))
+
+        list1 = keep.tile([P, S // 16], U16, name="list1")
+        list2 = keep.tile([P, M // 16], U16, name="list2")
+        nc.sync.dma_start(list1[:], offs)
+
+        sc_win = keep.tile([P, T], U8, name="sc_win", tag="late", bufs=1, align_bytes=64)
+        nc.vector.memset(sc_win[0:64, :].bitcast(I32), 0)
+        nc.vector.memset(sc_win[64:80, :].bitcast(I32), 0)
+        nc.scalar.dma_start(sc_win[96:128, :].bitcast(I32), tab_scales[0:2].rearrange("a q t -> q a t").bitcast(I32))
+        nc.scalar.dma_start(sc_win[80:96, :].bitcast(I32), tab_scales[2].bitcast(I32))
+        nc.sync.dma_start(list2[:], offs2)
+
+        def load_table(a):
+            tag, bufs = ("late", 1) if a == 2 else ("big", 2)
+            tab = keep.tile([P, T], I32, name=f"tab{a}", tag=tag, bufs=bufs, align_bytes=64)
+            nc.sync.dma_start(tab[:], tab_words[a].rearrange("p t i -> p (t i)").bitcast(I32))
+            return tab
+
+        def load_w1(a):
+            raw = keep.tile([P, 2 * H], U8, name=f"w1raw{a}", tag="w1raw", bufs=2, align_bytes=64)
+            nc.sync.dma_start(raw[:].bitcast(I32), w1_words[a].bitcast(I32))
+            return raw
+
+        tabs = [load_table(0)]
+
+        w1s_raw = keep.tile([P, PASSES, H], U8, name="w1s_raw", align_bytes=64)
+        nc.gpsimd.memset(w1s_raw[:].rearrange("p a c -> p (a c)").bitcast(I32), 0)
+        for q in range(QUADS):
+            nc.gpsimd.dma_start(
+                w1s_raw[32 * q : 32 * q + 4, :, :].bitcast(I32),
+                w1_scales[:, 4 * q : 4 * q + 4, :].rearrange("a r c -> r a c").bitcast(I32),
+            )
+        moved = keep.tile([P, 2, S], U8, name="moved", align_bytes=64)
+        nc.vector.memset(moved[:].rearrange("p a c -> p (a c)").bitcast(I32), 0)
+        moved2 = keep.tile([P, S], U8, name="moved2", align_bytes=64)
+        nc.vector.memset(moved2[:].bitcast(I32), 0)
+
+        w1raw = [load_w1(0)]
+        tabs.append(load_table(1))
+        w1raw.append(load_w1(1))
+
+        sc_got = keep.tile([P, S], U8, name="sc_got", align_bytes=64)
+        nc.vector.tensor_copy(sc_got[:], sc_win[:].indirect(list1[:]))
+        for q in range(QUADS):
+            nc.scalar.dma_start(moved[32 * q : 32 * q + 4, :, :].bitcast(I32), sc_got[96 + 8 * q : 104 + 8 * q, :].bitcast(I32))
+        tabs.append(load_table(2))
+        for q in range(QUADS):
+            nc.sync.dma_start(moved2[32 * q : 32 * q + 4, :].bitcast(I32), sc_got[80 + 4 * q : 84 + 4 * q, :].bitcast(I32))
+
+        w1s = []
+
+        def deal_scales(a, engine):
+            dealt = keep.tile([P, H], U8, name=f"w1s{a}", align_bytes=64)
+            engine.tensor_copy(
+                dealt[:].rearrange("p (b i m) -> p b i m", b=GROUPS, i=PACK),
+                w1s_raw[:, a, :].rearrange("p (b m i) -> p b i m", b=GROUPS, i=PACK),
+            )
+            w1s.append(dealt)
+
+        deal_scales(0, nc.vector)
+        deal_scales(1, nc.gpsimd)
+        deal_scales(2, nc.gpsimd)
+        gains = keep.tile([P, GROUPS, PACK], F32, name="gains")
+        nc.gpsimd.dma_start(gains[:], gain.rearrange("(b p i) -> p b i", p=P, i=PACK))
+
+        got = {}
+        w1c = {}
+
+        def gather_words(a, hf):
+            words = keep.tile([P, BANK], U32, name=f"got{a}{hf}", align_bytes=64)
+            cols = slice(hf * BANK // 16, (hf + 1) * BANK // 16)
+            nc.vector.tensor_copy(words[:], tabs[a][:].bitcast(U32).indirect(list1[:, cols]))
+            got[a, hf] = words
+
+        def deal_words(a, b):
+            dealt = keep.tile([P, 2 * BANK], U8, name=f"w1c{a}{b}", align_bytes=64)
+            nc.scalar.copy(
+                dealt[:].bitcast(U16).rearrange("p (i m) -> p i m", i=PACK),
+                w1raw[a][:].bitcast(U16)[:, b * BANK : (b + 1) * BANK].rearrange("p (m i) -> p i m", i=PACK),
+            )
+            w1c[a, b] = dealt
+
+        def first_product(bank, a, b, i, hf):
+            cols = slice(hf * BANK, (hf + 1) * BANK)
+            nc.tensor.matmul_mx(
+                out=bank[:],
+                lhsT=w1c[a, b][:, 2 * P * i : 2 * P * (i + 1)].bitcast(E2M1),
+                lhsT_scale=w1s[a][:, b * BANK + P * i : b * BANK + P * (i + 1)],
+                rhs=got[a, hf][:].bitcast(E4M3),
+                rhs_scale=moved[:, a, cols] if a < 2 else moved2[:, cols],
+                start=(a == 0),
+                stop=(a == PASSES - 1),
+            )
+
+        banks = {}
+        for hf in range(HALVES):
+            for i in range(PACK):
+                banks[0, i, hf] = psum.tile([P, BANK], F32, name=f"bank0{i}{hf}", tag="bank")
+        for a in range(PASSES):
+            if a == 2:
+                w1raw.append(load_w1(2))
+            deal_words(a, 0)
+            for hf in range(HALVES):
+                gather_words(a, hf)
+                for i in range(PACK):
+                    first_product(banks[0, i, hf], a, 0, i, hf)
+        for a in range(PASSES):
+            deal_words(a, 1)
+
+        w2raw = []
+        for b in range(GROUPS):
+            raw = keep.tile([P, T], I32, name=f"w2raw{b}", tag="big", bufs=2, align_bytes=64)
+            nc.sync.dma_start(raw[:].bitcast(F32), w2[b * 512 : (b + 1) * 512, :].rearrange("(p j) n -> p (j n)", j=PACK))
+            w2raw.append(raw)
+
+        w2h = []
+
+        def round_w2(b):
+            rounded = keep.tile([P, PACK * N], BF16, name=f"w2h{b}", align_bytes=64)
+            dst = rounded[:].rearrange("p (t m j) -> p m t j", t=PACK, j=PACK)
+            src = w2raw[b][:].bitcast(F32).rearrange("p (j m t) -> p m t j", j=PACK, t=PACK)
+            for c in range(4):
+                nc.gpsimd.tensor_scalar(
+                    dst[:, 32 * c : 32 * (c + 1)], src[:, 32 * c : 32 * (c + 1)], 1.0, 0.0, ALU.mult, ALU.add
+                )
+            w2h.append(rounded)
+
+        def quantize(name, src, width):
+            codes = keep.tile([P, width], U32, name=name + "_codes", align_bytes=64)
+            scales = keep.tile([P, width], U8, name=name + "_scales", align_bytes=64)
+            nc.vector.quantize_mx(out=codes[:].bitcast(E4M3), scales=scales[:], in_=src)
+            return codes, scales
+
+        looked = [keep.tile([P, PACK, M], F32, name=f"looked{b}") for b in range(GROUPS)]
+
+        def look(b, i, pieces):
+            h = keep.tile([P, S], F32, name=f"h{b}{i}", align_bytes=64)
+            tops = keep.tile([P, HALVES], F32, name=f"tops{b}{i}")
+            for hf in range(HALVES):
+                nc.vector.tensor_scalar(
+                    h[:, hf * BANK : (hf + 1) * BANK], banks[b, i, hf][:], 1.0, None, ALU.mult, ALU.max,
+                    accum_out=tops[:, hf : hf + 1],
+                )
+            neg_top = keep.tile([P, 1], F32, name=f"neg_top{b}{i}")
+            nc.vector.tensor_scalar(neg_top[:], tops[:, 0:1], tops[:, 1:2], -1.0, ALU.max, ALU.mult)
+            width = M // pieces
+            for c in range(pieces):
+                nc.scalar.activation(
+                    out=looked[b][:, i, c * width : (c + 1) * width],
+                    in_=h[:].indirect(list2[:, c * width // 16 : (c + 1) * width // 16]),
+                    func=ACT.Exp,
+                    bias=neg_top[:],
+                )
+
+        def apply_gain(engine, name, b, m0, width):
+            rounded = keep.tile([P, PACK * width], BF16, name=name, align_bytes=64)
+            engine.tensor_tensor(
+                rounded[:].rearrange("p (c e i) -> p c i e", e=4, i=PACK),
+                looked[b][:, :, m0 : m0 + width].rearrange("p i (c e) -> p c i e", e=4),
+                gains[:, b, :].unsqueeze(1).unsqueeze(3).to_broadcast([P, width // 4, PACK, 4]),
+                ALU.mult,
+            )
+            return rounded
+
+        b0_rows = keep.tile([P, PACK, M], BF16, name="b0_rows", align_bytes=64)
+
+        def gain_rows(i):
+            if i % 2:
+                nc.scalar.activation(out=b0_rows[:, i, :], in_=looked[0][:, i, :], func=ACT.Copy, scale=gains[:, 0, i : i + 1])
+            else:
+                nc.gpsimd.tensor_scalar(b0_rows[:, i, :], looked[0][:, i, :], gains[:, 0, i : i + 1], 0.0, ALU.mult, ALU.add)
+
+        round_w2(0)
+        for i in range(PACK):
+            look(0, i, 1)
+            if i % 2:
+                gain_rows(i)
+            for hf in range(HALVES):
+                banks[1, i, hf] = psum.tile([P, BANK], F32, name=f"bank1{i}{hf}", tag="bank")
+                for a in range(PASSES):
+                    first_product(banks[1, i, hf], a, 1, i, hf)
+        round_w2(1)
+        gain_rows(0)
+        gain_rows(2)
+        b0 = keep.tile([P, PACK * M], BF16, name="b0", align_bytes=64)
+        nc.gpsimd.tensor_scalar(
+            b0[:].rearrange("p (m i) -> p m i", i=PACK), b0_rows[:].rearrange("p i m -> p m i"), 1.0, 0.0, ALU.mult, ALU.add
+        )
+        for i in range(PACK):
+            look(1, i, 2 if i == PACK - 1 else 1)
+
+        w2q = [quantize(f"w2q{b}", w2h[b][:], N) for b in range(GROUPS)]
+        b0q = quantize("b0q", b0[:], M)
+
+        ybanks = [psum.tile([P, PACK, MQ], F32, name=f"ybank{c}", tag="bank") for c in range(M // MQ)]
+
+        def second_product(c, b, operand, m0):
+            codes, scales = operand
+            for t in range(PACK):
+                nc.tensor.matmul_mx(
+                    out=ybanks[c][:, t, :],
+                    lhsT=w2q[b][0][:, P * t : P * (t + 1)].bitcast(E4M3),
+                    lhsT_scale=w2q[b][1][:, P * t : P * (t + 1)],
+                    rhs=codes[:, m0 : m0 + MQ].bitcast(E4M3),
+                    rhs_scale=scales[:, m0 : m0 + MQ],
+                    start=(b == 0 and t == 0),
+                    stop=(b == GROUPS - 1 and t == PACK - 1),
+                )
+
+        for c in range(M // MQ):
+            second_product(c, 0, b0q, c * MQ)
+
+        y_codes = keep.tile([P, M], U32, name="y_codes", align_bytes=64)
+        y_scales = keep.tile([P, M], U8, name="y_scales", align_bytes=64)
+        out_rows = out_0.rearrange("(p t) m -> p t m", t=PACK)
+        out_words = out_1[0].rearrange("p m t -> p (m t)").bitcast(I32)
+        half = M // 2
+        b1q = []
+        for u in range(2):
+            b1 = apply_gain(nc.vector, f"b1{u}", 1, u * half, half)
+            b1q.append(quantize(f"b1q{u}", b1[:], half))
+            for c in range(2 * u, 2 * u + 2):
+                second_product(c, 1, b1q[u], (c % 2) * MQ)
+        for u in range(2):
+            y_round = keep.tile([P, PACK * half], BF16, name=f"y_round{u}", align_bytes=64)
+            for c in range(2 * u, 2 * u + 2):
+                y = keep.tile([P, PACK, MQ], F32, name=f"y{c}")
+                nc.scalar.copy(y[:], ybanks[c][:])
+                nc.sync.dma_start(out_rows[:, :, c * MQ : (c + 1) * MQ], y[:])
+                nc.vector.tensor_copy(
+                    y_round[:, (c % 2) * PACK * MQ : (c % 2 + 1) * PACK * MQ].rearrange("p (c e t) -> p c t e", e=4, t=PACK),
+                    y[:].rearrange("p t (c e) -> p c t e", e=4),
+                )
+            cols = slice(u * half, (u + 1) * half)
+            nc.vector.quantize_mx(out=y_codes[:, cols].bitcast(E4M3), scales=y_scales[:, cols], in_=y_round[:])
+            nc.sync.dma_start(out_words[:, cols], y_codes[:, cols].bitcast(I32))
+        for q in range(QUADS):
+            queue = nc.sync if q % 2 == 0 else nc.scalar
+            queue.dma_start(out_2[0, 4 * q : 4 * q + 4, :].bitcast(I32), y_scales[32 * q : 32 * q + 4, :].bitcast(I32))

@@ -32,86 +32,79 @@ def tile_list_talker_locator_kernel(
     nc = tc.nc
     with ExitStack() as ctx:
         keep = ctx.enter_context(tc.tile_pool(name="keep", bufs=1))
-        psum = ctx.enter_context(tc.psum_pool(name="psum", bufs=8))
+        late = ctx.enter_context(tc.tile_pool(name="late", bufs=1))
+        wide = ctx.enter_context(tc.tile_pool(name="wide", bufs=1))
+        psum = ctx.enter_context(tc.psum_pool(name="psum", bufs=1))
 
         list1 = keep.tile([P, S // 16], U16, name="list1")
         list2 = keep.tile([P, M // 16], U16, name="list2")
         nc.sync.dma_start(list1[:], offs)
 
-        sc_win = keep.tile([P, T], U8, name="sc_win", tag="late", bufs=1, align_bytes=64)
-        nc.vector.memset(sc_win[0:64, :].bitcast(I32), 0)
-        nc.vector.memset(sc_win[64:80, :].bitcast(I32), 0)
-        nc.scalar.dma_start(sc_win[96:128, :].bitcast(I32), tab_scales[0:2].rearrange("a q t -> q a t").bitcast(I32))
-        nc.scalar.dma_start(sc_win[80:96, :].bitcast(I32), tab_scales[2].bitcast(I32))
-        nc.sync.dma_start(list2[:], offs2)
+        sc_win = keep.tile([P, T], U8, name="sc_win", align_bytes=64)
+        w1s_raw = keep.tile([P, H], U8, name="w1s_raw", align_bytes=64)
+        for tile, rows in ((w1s_raw, w1_scales), (sc_win, tab_scales)):
+            nc.sync.dma_start(tile[96:128, :].bitcast(I32), rows[0:2].rearrange("a q t -> q a t").bitcast(I32))
+            nc.scalar.dma_start(tile[80:96, :].bitcast(I32), rows[2].bitcast(I32))
+        for rows in (slice(0, 64), slice(64, 80)):
+            nc.gpsimd.memset(w1s_raw[rows, :].bitcast(I32), 0)
+            nc.vector.memset(sc_win[rows, :].bitcast(I32), 0)
 
-        def load_table(a):
-            tag, bufs = ("late", 1) if a == 2 else ("big", 2)
-            tab = keep.tile([P, T], I32, name=f"tab{a}", tag=tag, bufs=bufs, align_bytes=64)
+        def load_table(a, tab):
             nc.sync.dma_start(tab[:], tab_words[a].rearrange("p t i -> p (t i)").bitcast(I32))
             return tab
 
-        def load_w1(a):
-            raw = keep.tile([P, 2 * H], U8, name=f"w1raw{a}", tag="w1raw", bufs=2, align_bytes=64)
-            nc.sync.dma_start(raw[:].bitcast(I32), w1_words[a].bitcast(I32))
+        def load_w1(b, raw):
+            nc.sync.dma_start(
+                raw[:].bitcast(I32), w1_words[:, :, 2 * BANK * b : 2 * BANK * (b + 1)].rearrange("a p c -> p a c").bitcast(I32)
+            )
             return raw
 
-        tabs = [load_table(0)]
+        tabs = [load_table(0, wide.tile([P, T], I32, name="tab0", align_bytes=64, offset=0))]
+        w1raw = [load_w1(0, keep.tile([P, PASSES, 2 * BANK], U8, name="w1raw0", align_bytes=64))]
+        tabs.append(load_table(1, wide.tile([P, T], I32, name="tab1", align_bytes=64, offset=4 * T)))
+        nc.sync.dma_start(list2[:], offs2)
 
-        w1s_raw = keep.tile([P, PASSES, H], U8, name="w1s_raw", align_bytes=64)
-        nc.gpsimd.memset(w1s_raw[:].rearrange("p a c -> p (a c)").bitcast(I32), 0)
-        for q in range(QUADS):
-            nc.gpsimd.dma_start(
-                w1s_raw[32 * q : 32 * q + 4, :, :].bitcast(I32),
-                w1_scales[:, 4 * q : 4 * q + 4, :].rearrange("a r c -> r a c").bitcast(I32),
-            )
-        moved = keep.tile([P, 2, S], U8, name="moved", align_bytes=64)
-        nc.vector.memset(moved[:].rearrange("p a c -> p (a c)").bitcast(I32), 0)
-        moved2 = keep.tile([P, S], U8, name="moved2", align_bytes=64)
+        moved = keep.tile([P, 2, S + H], U8, name="moved", align_bytes=64)
+        nc.gpsimd.memset(moved[:].rearrange("p a c -> p (a c)").bitcast(I32), 0)
+        moved2 = keep.tile([P, S + H], U8, name="moved2", align_bytes=64)
         nc.vector.memset(moved2[:].bitcast(I32), 0)
 
-        w1raw = [load_w1(0)]
-        tabs.append(load_table(1))
-        w1raw.append(load_w1(1))
-
-        sc_got = keep.tile([P, S], U8, name="sc_got", align_bytes=64)
+        staged = keep.tile([P, S + H], U8, name="staged", align_bytes=64)
+        nc.gpsimd.tensor_copy(
+            staged[:, S:].rearrange("p (b i m) -> p b i m", b=GROUPS, i=PACK),
+            w1s_raw[:].rearrange("p (b m i) -> p b i m", b=GROUPS, i=PACK),
+        )
+        sc_got = late.tile([P, S], U8, name="sc_got", align_bytes=64, offset=4 * T - S // 2)
         nc.vector.tensor_copy(sc_got[:], sc_win[:].indirect(list1[:]))
+        nc.vector.tensor_copy(staged[:, :S].bitcast(I32), sc_got[:].bitcast(I32))
         for q in range(QUADS):
-            nc.scalar.dma_start(moved[32 * q : 32 * q + 4, :, :].bitcast(I32), sc_got[96 + 8 * q : 104 + 8 * q, :].bitcast(I32))
-        tabs.append(load_table(2))
+            nc.sync.dma_start(moved[32 * q : 32 * q + 4, :, :].bitcast(I32), staged[96 + 8 * q : 104 + 8 * q, :].bitcast(I32))
+        tabs.append(load_table(2, late.tile([P, T], I32, name="tab2", align_bytes=64, offset=0)))
+        w1raw.append(load_w1(1, late.tile([P, PASSES, 2 * BANK], U8, name="w1raw1", align_bytes=64, offset=4 * T)))
         for q in range(QUADS):
-            nc.sync.dma_start(moved2[32 * q : 32 * q + 4, :].bitcast(I32), sc_got[80 + 4 * q : 84 + 4 * q, :].bitcast(I32))
+            nc.sync.dma_start(moved2[32 * q : 32 * q + 4, :].bitcast(I32), staged[80 + 4 * q : 84 + 4 * q, :].bitcast(I32))
+        planes = [moved[:, 0, :], moved[:, 1, :], moved2[:]]
 
-        w1s = []
-
-        def deal_scales(a, engine):
-            dealt = keep.tile([P, H], U8, name=f"w1s{a}", align_bytes=64)
-            engine.tensor_copy(
-                dealt[:].rearrange("p (b i m) -> p b i m", b=GROUPS, i=PACK),
-                w1s_raw[:, a, :].rearrange("p (b m i) -> p b i m", b=GROUPS, i=PACK),
-            )
-            w1s.append(dealt)
-
-        deal_scales(0, nc.vector)
-        deal_scales(1, nc.gpsimd)
-        deal_scales(2, nc.gpsimd)
         gains = keep.tile([P, GROUPS, PACK], F32, name="gains")
         nc.gpsimd.dma_start(gains[:], gain.rearrange("(b p i) -> p b i", p=P, i=PACK))
 
         got = {}
         w1c = {}
 
-        def gather_words(a, hf):
-            words = keep.tile([P, BANK], U32, name=f"got{a}{hf}", align_bytes=64)
-            cols = slice(hf * BANK // 16, (hf + 1) * BANK // 16)
-            nc.vector.tensor_copy(words[:], tabs[a][:].bitcast(U32).indirect(list1[:, cols]))
-            got[a, hf] = words
+        def gather_words(a, pieces):
+            width = S // pieces
+            for c in range(pieces):
+                words = keep.tile([P, width], U32, name=f"got{a}{c}", align_bytes=64)
+                cols = slice(c * width // 16, (c + 1) * width // 16)
+                nc.vector.tensor_copy(words[:], tabs[a][:].bitcast(U32).indirect(list1[:, cols]))
+                for u in range(width // BANK):
+                    got[a, c * width // BANK + u] = words[:, u * BANK : (u + 1) * BANK]
 
         def deal_words(a, b):
             dealt = keep.tile([P, 2 * BANK], U8, name=f"w1c{a}{b}", align_bytes=64)
             nc.scalar.copy(
                 dealt[:].bitcast(U16).rearrange("p (i m) -> p i m", i=PACK),
-                w1raw[a][:].bitcast(U16)[:, b * BANK : (b + 1) * BANK].rearrange("p (m i) -> p i m", i=PACK),
+                w1raw[b][:, a, :].bitcast(U16).rearrange("p (m i) -> p i m", i=PACK),
             )
             w1c[a, b] = dealt
 
@@ -120,43 +113,50 @@ def tile_list_talker_locator_kernel(
             nc.tensor.matmul_mx(
                 out=bank[:],
                 lhsT=w1c[a, b][:, 2 * P * i : 2 * P * (i + 1)].bitcast(E2M1),
-                lhsT_scale=w1s[a][:, b * BANK + P * i : b * BANK + P * (i + 1)],
-                rhs=got[a, hf][:].bitcast(E4M3),
-                rhs_scale=moved[:, a, cols] if a < 2 else moved2[:, cols],
+                lhsT_scale=planes[a][:, S + b * BANK + P * i : S + b * BANK + P * (i + 1)],
+                rhs=got[a, hf].bitcast(E4M3),
+                rhs_scale=planes[a][:, cols],
                 start=(a == 0),
                 stop=(a == PASSES - 1),
             )
 
         banks = {}
-        for hf in range(HALVES):
-            for i in range(PACK):
-                banks[0, i, hf] = psum.tile([P, BANK], F32, name=f"bank0{i}{hf}", tag="bank")
         for a in range(PASSES):
-            if a == 2:
-                w1raw.append(load_w1(2))
             deal_words(a, 0)
-            for hf in range(HALVES):
-                gather_words(a, hf)
-                for i in range(PACK):
-                    first_product(banks[0, i, hf], a, 0, i, hf)
+        for a in range(PASSES):
+            gather_words(a, 1 if a == 1 else HALVES)
         for a in range(PASSES):
             deal_words(a, 1)
 
-        w2raw = []
+        def open_bank(b, i, hf):
+            banks[b, i, hf] = psum.tile([P, BANK], F32, name=f"bank{b}{i}{hf}", tag="h", bufs=5)
+
+        early = [(i, hf) for i in range(PACK) for hf in range(HALVES)][:5]
+        for i, hf in early:
+            open_bank(0, i, hf)
+        for a in range(PASSES):
+            for i, hf in early:
+                first_product(banks[0, i, hf], a, 0, i, hf)
+        waiting = [(b, i, hf) for b in range(GROUPS) for i in range(PACK) for hf in range(HALVES)][5:]
+
+        w2raw = {}
         for b in range(GROUPS):
-            raw = keep.tile([P, T], I32, name=f"w2raw{b}", tag="big", bufs=2, align_bytes=64)
-            nc.sync.dma_start(raw[:].bitcast(F32), w2[b * 512 : (b + 1) * 512, :].rearrange("(p j) n -> p (j n)", j=PACK))
-            w2raw.append(raw)
+            for u in range(2):
+                raw = wide.tile([P, PACK, N // 2], F32, name=f"w2raw{b}{u}", align_bytes=64, offset=4 * T * b + 2 * T * u)
+                nc.sync.dma_start(
+                    raw[:], w2[b * 512 : (b + 1) * 512, u * N // 2 : (u + 1) * N // 2].rearrange("(p j) n -> p j n", j=PACK)
+                )
+                w2raw[b, u] = raw
 
         w2h = []
 
         def round_w2(b):
             rounded = keep.tile([P, PACK * N], BF16, name=f"w2h{b}", align_bytes=64)
             dst = rounded[:].rearrange("p (t m j) -> p m t j", t=PACK, j=PACK)
-            src = w2raw[b][:].bitcast(F32).rearrange("p (j m t) -> p m t j", j=PACK, t=PACK)
             for c in range(4):
+                src = w2raw[b, c // 2][:].rearrange("p j (m t) -> p m t j", t=PACK)
                 nc.gpsimd.tensor_scalar(
-                    dst[:, 32 * c : 32 * (c + 1)], src[:, 32 * c : 32 * (c + 1)], 1.0, 0.0, ALU.mult, ALU.add
+                    dst[:, 32 * c : 32 * (c + 1)], src[:, 32 * (c % 2) : 32 * (c % 2 + 1)], 1.0, 0.0, ALU.mult, ALU.add
                 )
             w2h.append(rounded)
 
@@ -168,16 +168,21 @@ def tile_list_talker_locator_kernel(
 
         looked = [keep.tile([P, PACK, M], F32, name=f"looked{b}") for b in range(GROUPS)]
 
-        def look(b, i, pieces):
-            h = keep.tile([P, S], F32, name=f"h{b}{i}", align_bytes=64)
+        def look(b, i, pieces, rows=None):
+            h = keep.tile([P, S], F32, name=f"h{b}{i}", tag=f"h{b}{i}", align_bytes=64)
             tops = keep.tile([P, HALVES], F32, name=f"tops{b}{i}")
             for hf in range(HALVES):
                 nc.vector.tensor_scalar(
                     h[:, hf * BANK : (hf + 1) * BANK], banks[b, i, hf][:], 1.0, None, ALU.mult, ALU.max,
                     accum_out=tops[:, hf : hf + 1],
                 )
+                if waiting:
+                    place = waiting.pop(0)
+                    open_bank(*place)
+                    for a in range(PASSES):
+                        first_product(banks[place], a, *place)
             neg_top = keep.tile([P, 1], F32, name=f"neg_top{b}{i}")
-            nc.vector.tensor_scalar(neg_top[:], tops[:, 0:1], tops[:, 1:2], -1.0, ALU.max, ALU.mult)
+            nc.vector.tensor_reduce(neg_top[:], tops[:], mybir.AxisListType.X, ALU.max, negate=True)
             width = M // pieces
             for c in range(pieces):
                 nc.scalar.activation(
@@ -186,48 +191,35 @@ def tile_list_talker_locator_kernel(
                     func=ACT.Exp,
                     bias=neg_top[:],
                 )
-
-        def apply_gain(engine, name, b, m0, width):
-            rounded = keep.tile([P, PACK * width], BF16, name=name, align_bytes=64)
-            engine.tensor_tensor(
-                rounded[:].rearrange("p (c e i) -> p c i e", e=4, i=PACK),
-                looked[b][:, :, m0 : m0 + width].rearrange("p i (c e) -> p c i e", e=4),
-                gains[:, b, :].unsqueeze(1).unsqueeze(3).to_broadcast([P, width // 4, PACK, 4]),
-                ALU.mult,
-            )
-            return rounded
+                if rows is not None:
+                    cols = slice(c * width, (c + 1) * width)
+                    nc.scalar.activation(out=rows[:, i, cols], in_=looked[b][:, i, cols], func=ACT.Copy, scale=gains[:, b, i : i + 1])
 
         b0_rows = keep.tile([P, PACK, M], BF16, name="b0_rows", align_bytes=64)
-
-        def gain_rows(i):
-            if i % 2:
-                nc.scalar.activation(out=b0_rows[:, i, :], in_=looked[0][:, i, :], func=ACT.Copy, scale=gains[:, 0, i : i + 1])
-            else:
-                nc.gpsimd.tensor_scalar(b0_rows[:, i, :], looked[0][:, i, :], gains[:, 0, i : i + 1], 0.0, ALU.mult, ALU.add)
-
         round_w2(0)
         for i in range(PACK):
             look(0, i, 1)
             if i % 2:
-                gain_rows(i)
-            for hf in range(HALVES):
-                banks[1, i, hf] = psum.tile([P, BANK], F32, name=f"bank1{i}{hf}", tag="bank")
-                for a in range(PASSES):
-                    first_product(banks[1, i, hf], a, 1, i, hf)
+                nc.scalar.activation(out=b0_rows[:, i, :], in_=looked[0][:, i, :], func=ACT.Copy, scale=gains[:, 0, i : i + 1])
+            else:
+                nc.gpsimd.tensor_scalar(b0_rows[:, i, :], looked[0][:, i, :], gains[:, 0, i : i + 1], 0.0, ALU.mult, ALU.add)
         round_w2(1)
-        gain_rows(0)
-        gain_rows(2)
-        b0 = keep.tile([P, PACK * M], BF16, name="b0", align_bytes=64)
-        nc.gpsimd.tensor_scalar(
-            b0[:].rearrange("p (m i) -> p m i", i=PACK), b0_rows[:].rearrange("p i m -> p m i"), 1.0, 0.0, ALU.mult, ALU.add
-        )
-        for i in range(PACK):
-            look(1, i, 2 if i == PACK - 1 else 1)
-
-        w2q = [quantize(f"w2q{b}", w2h[b][:], N) for b in range(GROUPS)]
+        w2q = [quantize("w2q0", w2h[0][:], N)]
+        b1_rows = keep.tile([P, PACK, M], BF16, name="b1_rows", align_bytes=64)
+        for i in range(PACK - 1):
+            look(1, i, 1)
+            nc.gpsimd.tensor_scalar(b1_rows[:, i, :], looked[1][:, i, :], gains[:, 1, i : i + 1], 0.0, ALU.mult, ALU.add)
+            if i == 1:
+                b0 = keep.tile([P, PACK * M], BF16, name="b0", align_bytes=64)
+                nc.vector.tensor_copy(
+                    b0[:].rearrange("p (c e i) -> p c i e", e=4, i=PACK), b0_rows[:].rearrange("p i (c e) -> p c i e", e=4)
+                )
+        look(1, PACK - 1, 2, b1_rows)
         b0q = quantize("b0q", b0[:], M)
+        w2q.append(quantize("w2q1", w2h[1][:], N))
 
-        ybanks = [psum.tile([P, PACK, MQ], F32, name=f"ybank{c}", tag="bank") for c in range(M // MQ)]
+        ybanks = [psum.tile([P, PACK, MQ], F32, name=f"ybank{c}", tag="y", bufs=3) for c in range(3)]
+        ybanks.append(psum.tile([P, PACK, MQ], F32, name="ybank3", tag="h", bufs=5))
 
         def second_product(c, b, operand, m0):
             codes, scales = operand
@@ -249,26 +241,29 @@ def tile_list_talker_locator_kernel(
         y_scales = keep.tile([P, M], U8, name="y_scales", align_bytes=64)
         out_rows = out_0.rearrange("(p t) m -> p t m", t=PACK)
         out_words = out_1[0].rearrange("p m t -> p (m t)").bitcast(I32)
-        half = M // 2
-        b1q = []
-        for u in range(2):
-            b1 = apply_gain(nc.vector, f"b1{u}", 1, u * half, half)
-            b1q.append(quantize(f"b1q{u}", b1[:], half))
-            for c in range(2 * u, 2 * u + 2):
-                second_product(c, 1, b1q[u], (c % 2) * MQ)
-        for u in range(2):
-            y_round = keep.tile([P, PACK * half], BF16, name=f"y_round{u}", align_bytes=64)
-            for c in range(2 * u, 2 * u + 2):
-                y = keep.tile([P, PACK, MQ], F32, name=f"y{c}")
-                nc.scalar.copy(y[:], ybanks[c][:])
-                nc.sync.dma_start(out_rows[:, :, c * MQ : (c + 1) * MQ], y[:])
+        for c in range(M // MQ):
+            b1 = keep.tile([P, PACK * MQ], BF16, name=f"b1{c}", align_bytes=64)
+            nc.vector.tensor_copy(
+                b1[:].rearrange("p (c e i) -> p c i e", e=4, i=PACK),
+                b1_rows[:, :, c * MQ : (c + 1) * MQ].rearrange("p i (c e) -> p c i e", e=4),
+            )
+            second_product(c, 1, quantize(f"b1q{c}", b1[:], MQ), 0)
+        for c in range(M // MQ):
+            cols = slice(c * MQ, (c + 1) * MQ)
+            y = keep.tile([P, PACK, MQ], F32, name=f"y{c}")
+            y_round = keep.tile([P, PACK * MQ], BF16, name=f"y_round{c}", align_bytes=64)
+            if c == 3:
+                nc.scalar.copy(y_round[:].rearrange("p (m t) -> p m t", t=PACK), ybanks[c][:].rearrange("p t m -> p m t"))
+            nc.scalar.copy(y[:], ybanks[c][:])
+            nc.sync.dma_start(out_rows[:, :, cols], y[:])
+            if c < 3:
                 nc.vector.tensor_copy(
-                    y_round[:, (c % 2) * PACK * MQ : (c % 2 + 1) * PACK * MQ].rearrange("p (c e t) -> p c t e", e=4, t=PACK),
-                    y[:].rearrange("p t (c e) -> p c t e", e=4),
+                    y_round[:].rearrange("p (c e t) -> p c t e", e=4, t=PACK), y[:].rearrange("p t (c e) -> p c t e", e=4)
                 )
-            cols = slice(u * half, (u + 1) * half)
             nc.vector.quantize_mx(out=y_codes[:, cols].bitcast(E4M3), scales=y_scales[:, cols], in_=y_round[:])
-            nc.sync.dma_start(out_words[:, cols], y_codes[:, cols].bitcast(I32))
+            if c % 2:
+                pair = slice((c - 1) * MQ, (c + 1) * MQ)
+                nc.sync.dma_start(out_words[:, pair], y_codes[:, pair].bitcast(I32))
         for q in range(QUADS):
             queue = nc.sync if q % 2 == 0 else nc.scalar
             queue.dma_start(out_2[0, 4 * q : 4 * q + 4, :].bitcast(I32), y_scales[32 * q : 32 * q + 4, :].bitcast(I32))

@@ -70,7 +70,7 @@ def tile_list_talker_locator_kernel(
         nc.vector.memset(moved2[:].bitcast(I32), 0)
 
         staged = keep.tile([P, S + H], U8, name="staged", align_bytes=64)
-        nc.gpsimd.tensor_copy(
+        nc.vector.tensor_copy(
             staged[:, S:].rearrange("p (b i m) -> p b i m", b=GROUPS, i=PACK),
             w1s_raw[:].rearrange("p (b m i) -> p b i m", b=GROUPS, i=PACK),
         )
@@ -86,7 +86,7 @@ def tile_list_talker_locator_kernel(
         planes = [moved[:, 0, :], moved[:, 1, :], moved2[:]]
 
         gains = keep.tile([P, GROUPS, PACK], F32, name="gains")
-        nc.gpsimd.dma_start(gains[:], gain.rearrange("(b p i) -> p b i", p=P, i=PACK))
+        nc.scalar.dma_start(gains[:], gain.rearrange("(b p i) -> p b i", p=P, i=PACK))
 
         got = {}
         w1c = {}
@@ -148,17 +148,12 @@ def tile_list_talker_locator_kernel(
                 )
                 w2raw[b, u] = raw
 
-        w2h = []
+        w2h = [keep.tile([P, PACK * N], BF16, name=f"w2h{b}", align_bytes=64) for b in range(GROUPS)]
 
-        def round_w2(b):
-            rounded = keep.tile([P, PACK * N], BF16, name=f"w2h{b}", align_bytes=64)
-            dst = rounded[:].rearrange("p (t m j) -> p m t j", t=PACK, j=PACK)
-            for c in range(4):
-                src = w2raw[b, c // 2][:].rearrange("p j (m t) -> p m t j", t=PACK)
-                nc.gpsimd.tensor_scalar(
-                    dst[:, 32 * c : 32 * (c + 1)], src[:, 32 * (c % 2) : 32 * (c % 2 + 1)], 1.0, 0.0, ALU.mult, ALU.add
-                )
-            w2h.append(rounded)
+        def round_w2(copy, b, m0, width):
+            dst = w2h[b][:].rearrange("p (t m j) -> p m t j", t=PACK, j=PACK)
+            src = w2raw[b, m0 // 64][:].rearrange("p j (m t) -> p m t j", t=PACK)
+            copy(dst[:, m0 : m0 + width], src[:, m0 % 64 : m0 % 64 + width])
 
         def quantize(name, src, width):
             codes = keep.tile([P, width], U32, name=name + "_codes", align_bytes=64)
@@ -196,27 +191,36 @@ def tile_list_talker_locator_kernel(
                     nc.scalar.activation(out=rows[:, i, cols], in_=looked[b][:, i, cols], func=ACT.Copy, scale=gains[:, b, i : i + 1])
 
         b0_rows = keep.tile([P, PACK, M], BF16, name="b0_rows", align_bytes=64)
-        round_w2(0)
+        b1_rows = keep.tile([P, PACK, M], BF16, name="b1_rows", align_bytes=64)
+        round_w2(nc.scalar.copy, 0, 0, 64)
+        round_w2(nc.scalar.copy, 0, 64, 32)
+        w2q = []
         for i in range(PACK):
             look(0, i, 1)
-            if i % 2:
-                nc.scalar.activation(out=b0_rows[:, i, :], in_=looked[0][:, i, :], func=ACT.Copy, scale=gains[:, 0, i : i + 1])
-            else:
-                nc.gpsimd.tensor_scalar(b0_rows[:, i, :], looked[0][:, i, :], gains[:, 0, i : i + 1], 0.0, ALU.mult, ALU.add)
-        round_w2(1)
-        w2q = [quantize("w2q0", w2h[0][:], N)]
-        b1_rows = keep.tile([P, PACK, M], BF16, name="b1_rows", align_bytes=64)
-        for i in range(PACK - 1):
+            nc.gpsimd.tensor_scalar(b0_rows[:, i, :], looked[0][:, i, :], gains[:, 0, i : i + 1], 0.0, ALU.mult, ALU.add)
+            if i == 0:
+                round_w2(nc.vector.tensor_copy, 0, 96, 32)
+            elif i < 3:
+                round_w2(nc.vector.tensor_copy, 1, 64 * (i - 1), 64)
+            if i in (1, 3):
+                w2q.append(quantize(f"w2q{i // 2}", w2h[i // 2][:], N))
+        look(1, 0, 1, b1_rows)
+        for i in range(1, PACK - 1):
             look(1, i, 1)
             nc.gpsimd.tensor_scalar(b1_rows[:, i, :], looked[1][:, i, :], gains[:, 1, i : i + 1], 0.0, ALU.mult, ALU.add)
-            if i == 1:
-                b0 = keep.tile([P, PACK * M], BF16, name="b0", align_bytes=64)
-                nc.vector.tensor_copy(
-                    b0[:].rearrange("p (c e i) -> p c i e", e=4, i=PACK), b0_rows[:].rearrange("p i (c e) -> p c i e", e=4)
-                )
+        b0 = keep.tile([P, PACK * M], BF16, name="b0", align_bytes=64)
+        for c in range(3):
+            cols = slice(c * MQ, (c + 1) * MQ)
+            nc.gpsimd.tensor_scalar(
+                b0[:].rearrange("p (m i) -> p m i", i=PACK)[:, cols], b0_rows[:].rearrange("p i m -> p m i")[:, cols],
+                1.0, 0.0, ALU.mult, ALU.add,
+            )
         look(1, PACK - 1, 2, b1_rows)
+        nc.vector.tensor_copy(
+            b0[:, 3 * PACK * MQ :].rearrange("p (c e i) -> p c i e", e=4, i=PACK),
+            b0_rows[:, :, 3 * MQ :].rearrange("p i (c e) -> p c i e", e=4),
+        )
         b0q = quantize("b0q", b0[:], M)
-        w2q.append(quantize("w2q1", w2h[1][:], N))
 
         ybanks = [psum.tile([P, PACK, MQ], F32, name=f"ybank{c}", tag="y", bufs=3) for c in range(3)]
         ybanks.append(psum.tile([P, PACK, MQ], F32, name="ybank3", tag="h", bufs=5))

@@ -77,11 +77,11 @@ def tile_list_talker_locator_kernel(
         sc_got = late.tile([P, S], U8, name="sc_got", align_bytes=64, offset=4 * T - S // 2)
         nc.vector.tensor_copy(sc_got[:], sc_win[:].indirect(list1[:]))
         nc.vector.tensor_copy(staged[:, :S].bitcast(I32), sc_got[:].bitcast(I32))
-        for q in range(QUADS):
+        for q in (0, 2, 1, 3):
             nc.sync.dma_start(moved[32 * q : 32 * q + 4, :, :].bitcast(I32), staged[96 + 8 * q : 104 + 8 * q, :].bitcast(I32))
         tabs.append(load_table(2, late.tile([P, T], I32, name="tab2", align_bytes=64, offset=0)))
         w1raw.append(load_w1(1, late.tile([P, PASSES, 2 * BANK], U8, name="w1raw1", align_bytes=64, offset=4 * T)))
-        for q in range(QUADS):
+        for q in (0, 2, 1, 3):
             nc.sync.dma_start(moved2[32 * q : 32 * q + 4, :].bitcast(I32), staged[80 + 4 * q : 84 + 4 * q, :].bitcast(I32))
         planes = [moved[:, 0, :], moved[:, 1, :], moved2[:]]
 
@@ -139,21 +139,21 @@ def tile_list_talker_locator_kernel(
                 first_product(banks[0, i, hf], a, 0, i, hf)
         waiting = [(b, i, hf) for b in range(GROUPS) for i in range(PACK) for hf in range(HALVES)][5:]
 
-        w2raw = {}
+        w2raw = []
         for b in range(GROUPS):
-            for u in range(2):
-                raw = wide.tile([P, PACK, N // 2], F32, name=f"w2raw{b}{u}", align_bytes=64, offset=4 * T * b + 2 * T * u)
-                nc.sync.dma_start(
-                    raw[:], w2[b * 512 : (b + 1) * 512, u * N // 2 : (u + 1) * N // 2].rearrange("(p j) n -> p j n", j=PACK)
-                )
-                w2raw[b, u] = raw
+            raw = wide.tile([P, PACK, N], F32, name=f"w2raw{b}", align_bytes=64, offset=4 * T * b)
+            nc.sync.dma_start(raw[:], w2[b * 512 : (b + 1) * 512, :].rearrange("(p j) n -> p j n", j=PACK))
+            w2raw.append(raw)
 
         w2h = [keep.tile([P, PACK * N], BF16, name=f"w2h{b}", align_bytes=64) for b in range(GROUPS)]
 
         def round_w2(copy, b, m0, width):
             dst = w2h[b][:].rearrange("p (t m j) -> p m t j", t=PACK, j=PACK)
-            src = w2raw[b, m0 // 64][:].rearrange("p j (m t) -> p m t j", t=PACK)
-            copy(dst[:, m0 : m0 + width], src[:, m0 % 64 : m0 % 64 + width])
+            src = w2raw[b][:].rearrange("p j (m t) -> p m t j", t=PACK)
+            copy(dst[:, m0 : m0 + width], src[:, m0 : m0 + width])
+
+        def pool_copy(dst, src):
+            nc.gpsimd.tensor_scalar(dst, src, 1.0, 0.0, ALU.mult, ALU.add)
 
         def quantize(name, src, width):
             codes = keep.tile([P, width], U32, name=name + "_codes", align_bytes=64)
@@ -192,22 +192,20 @@ def tile_list_talker_locator_kernel(
 
         b0_rows = keep.tile([P, PACK, M], BF16, name="b0_rows", align_bytes=64)
         b1_rows = keep.tile([P, PACK, M], BF16, name="b1_rows", align_bytes=64)
-        round_w2(nc.scalar.copy, 0, 0, 64)
-        round_w2(nc.scalar.copy, 0, 64, 32)
-        w2q = []
+        for c in range(4):
+            round_w2(pool_copy, 0, 32 * c, 32)
         for i in range(PACK):
             look(0, i, 1)
             nc.gpsimd.tensor_scalar(b0_rows[:, i, :], looked[0][:, i, :], gains[:, 0, i : i + 1], 0.0, ALU.mult, ALU.add)
-            if i == 0:
-                round_w2(nc.vector.tensor_copy, 0, 96, 32)
-            elif i < 3:
-                round_w2(nc.vector.tensor_copy, 1, 64 * (i - 1), 64)
-            if i in (1, 3):
-                w2q.append(quantize(f"w2q{i // 2}", w2h[i // 2][:], N))
+        round_w2(nc.vector.tensor_copy, 1, 0, 64)
         look(1, 0, 1, b1_rows)
+        round_w2(nc.vector.tensor_copy, 1, 64, 64)
+        w2q = [quantize("w2q0", w2h[0][:], N)]
         for i in range(1, PACK - 1):
             look(1, i, 1)
             nc.gpsimd.tensor_scalar(b1_rows[:, i, :], looked[1][:, i, :], gains[:, 1, i : i + 1], 0.0, ALU.mult, ALU.add)
+            if i == 1:
+                w2q.append(quantize("w2q1", w2h[1][:], N))
         b0 = keep.tile([P, PACK * M], BF16, name="b0", align_bytes=64)
         for c in range(3):
             cols = slice(c * MQ, (c + 1) * MQ)
@@ -217,8 +215,8 @@ def tile_list_talker_locator_kernel(
             )
         look(1, PACK - 1, 2, b1_rows)
         nc.vector.tensor_copy(
-            b0[:, 3 * PACK * MQ :].rearrange("p (c e i) -> p c i e", e=4, i=PACK),
-            b0_rows[:, :, 3 * MQ :].rearrange("p i (c e) -> p c i e", e=4),
+            b0[:, 3 * PACK * MQ :].rearrange("p (m i) -> p m i", i=PACK),
+            b0_rows[:, :, 3 * MQ :].rearrange("p i m -> p m i"),
         )
         b0q = quantize("b0q", b0[:], M)
 
@@ -248,8 +246,8 @@ def tile_list_talker_locator_kernel(
         for c in range(M // MQ):
             b1 = keep.tile([P, PACK * MQ], BF16, name=f"b1{c}", align_bytes=64)
             nc.vector.tensor_copy(
-                b1[:].rearrange("p (c e i) -> p c i e", e=4, i=PACK),
-                b1_rows[:, :, c * MQ : (c + 1) * MQ].rearrange("p i (c e) -> p c i e", e=4),
+                b1[:].rearrange("p (m i) -> p m i", i=PACK),
+                b1_rows[:, :, c * MQ : (c + 1) * MQ].rearrange("p i m -> p m i"),
             )
             second_product(c, 1, quantize(f"b1q{c}", b1[:], MQ), 0)
         for c in range(M // MQ):

@@ -69,8 +69,8 @@ def tile_list_talker_locator_kernel(
         moved2 = keep.tile([P, S + H], U8, name="moved2", align_bytes=64)
         nc.vector.memset(moved2[:].bitcast(I32), 0)
 
-        staged = keep.tile([P, S + H], U8, name="staged", align_bytes=64)
-        nc.vector.tensor_copy(
+        staged = keep.tile([P, S + H], U8, name="staged", tag="staged", align_bytes=64)
+        nc.gpsimd.tensor_copy(
             staged[:, S:].rearrange("p (b i m) -> p b i m", b=GROUPS, i=PACK),
             w1s_raw[:].rearrange("p (b m i) -> p b i m", b=GROUPS, i=PACK),
         )
@@ -85,7 +85,7 @@ def tile_list_talker_locator_kernel(
             nc.sync.dma_start(moved2[32 * q : 32 * q + 4, :].bitcast(I32), staged[80 + 4 * q : 84 + 4 * q, :].bitcast(I32))
         planes = [moved[:, 0, :], moved[:, 1, :], moved2[:]]
 
-        gains = keep.tile([P, GROUPS, PACK], F32, name="gains")
+        gains = keep.tile([P, GROUPS, PACK], F32, name="gains", tag="staged", align_bytes=64)
         nc.scalar.dma_start(gains[:], gain.rearrange("(b p i) -> p b i", p=P, i=PACK))
 
         got = {}
@@ -204,8 +204,6 @@ def tile_list_talker_locator_kernel(
         for i in range(1, PACK - 1):
             look(1, i, 1)
             nc.gpsimd.tensor_scalar(b1_rows[:, i, :], looked[1][:, i, :], gains[:, 1, i : i + 1], 0.0, ALU.mult, ALU.add)
-            if i == 1:
-                w2q.append(quantize("w2q1", w2h[1][:], N))
         b0 = keep.tile([P, PACK * M], BF16, name="b0", align_bytes=64)
         for c in range(3):
             cols = slice(c * MQ, (c + 1) * MQ)
@@ -218,6 +216,7 @@ def tile_list_talker_locator_kernel(
             b0[:, 3 * PACK * MQ :].rearrange("p (m i) -> p m i", i=PACK),
             b0_rows[:, :, 3 * MQ :].rearrange("p i m -> p m i"),
         )
+        w2q.append(quantize("w2q1", w2h[1][:], N))
         b0q = quantize("b0q", b0[:], M)
 
         ybanks = [psum.tile([P, PACK, MQ], F32, name=f"ybank{c}", tag="y", bufs=3) for c in range(3)]

from contextlib import ExitStack

import concourse.mybir as mybir

K, T, S, H, M, N = 1536, 2048, 1024, 1024, 512, 512
FLOPS = 2 * K * H * S + 2 * H * N * M

F32 = mybir.dt.float32
BF16 = mybir.dt.bfloat16
I32 = mybir.dt.int32
U32 = mybir.dt.uint32
U16 = mybir.dt.uint16
U8 = mybir.dt.uint8
E4M3 = mybir.dt.float8_e4m3fn_x4
E2M1 = mybir.dt.float4_e2m1fn_x4
ALU = mybir.AluOpType
ACT = mybir.ActivationFunctionType

P = 128
PACK = 4
PASSES = K // (P * PACK)
GROUPS = H // (P * PACK)
BANK = 512
HALVES = S // BANK
QUADS = 4
MQ = 128


def tile_list_talker_locator_kernel(
    tc, tab_words, tab_scales, offs, offs2, w1_words, w1_scales, gain, w2, out_0, out_1, out_2
):
    nc = tc.nc
    with ExitStack() as ctx:
        keep = ctx.enter_context(tc.tile_pool(name="keep", bufs=1))
        late = ctx.enter_context(tc.tile_pool(name="late", bufs=1))
        wide = ctx.enter_context(tc.tile_pool(name="wide", bufs=1))
        psum = ctx.enter_context(tc.psum_pool(name="psum", bufs=1))

        list1 = keep.tile([P, S // 16], U16, name="list1")
        list2 = keep.tile([P, M // 16], U16, name="list2")
        nc.sync.dma_start(list1[:], offs)

        sc_win = keep.tile([P, T], U8, name="sc_win", align_bytes=64)
        w1s_raw = keep.tile([P, H], U8, name="w1s_raw", align_bytes=64)
        for tile, rows in ((w1s_raw, w1_scales), (sc_win, tab_scales)):
            nc.sync.dma_start(tile[96:128, :].bitcast(I32), rows[0:2].rearrange("a q t -> q a t").bitcast(I32))
            nc.scalar.dma_start(tile[80:96, :].bitcast(I32), rows[2].bitcast(I32))
        for rows in (slice(0, 64), slice(64, 80)):
            nc.gpsimd.memset(w1s_raw[rows, :].bitcast(I32), 0)
            nc.vector.memset(sc_win[rows, :].bitcast(I32), 0)

        def load_table(a, tab):
            nc.sync.dma_start(tab[:], tab_words[a].rearrange("p t i -> p (t i)").bitcast(I32))
            return tab

        def load_w1(b, raw):
            nc.sync.dma_start(
                raw[:].bitcast(I32), w1_words[:, :, 2 * BANK * b : 2 * BANK * (b + 1)].rearrange("a p c -> p a c").bitcast(I32)
            )
            return raw

        tabs = [load_table(0, wide.tile([P, T], I32, name="tab0", align_bytes=64, offset=0))]
        w1raw = [load_w1(0, keep.tile([P, PASSES, 2 * BANK], U8, name="w1raw0", align_bytes=64))]
        tabs.append(load_table(1, wide.tile([P, T], I32, name="tab1", align_bytes=64, offset=4 * T)))
        nc.sync.dma_start(list2[:], offs2)

        moved = keep.tile([P, 2, S + H], U8, name="moved", align_bytes=64)
        nc.gpsimd.memset(moved[:].rearrange("p a c -> p (a c)").bitcast(I32), 0)
        moved2 = keep.tile([P, S + H], U8, name="moved2", align_bytes=64)
        nc.vector.memset(moved2[:].bitcast(I32), 0)

        staged = keep.tile([P, S + H], U8, name="staged", tag="staged", align_bytes=64)
        nc.gpsimd.tensor_copy(
            staged[:, S:].rearrange("p (b i m) -> p b i m", b=GROUPS, i=PACK),
            w1s_raw[:].rearrange("p (b m i) -> p b i m", b=GROUPS, i=PACK),
        )
        sc_got = late.tile([P, S], U8, name="sc_got", align_bytes=64, offset=4 * T - S // 2)
        nc.vector.tensor_copy(sc_got[:], sc_win[:].indirect(list1[:]))
        nc.vector.tensor_copy(staged[:, :S].bitcast(I32), sc_got[:].bitcast(I32))
        for q in (0, 2, 1, 3):
            nc.sync.dma_start(moved[32 * q : 32 * q + 4, :, :].bitcast(I32), staged[96 + 8 * q : 104 + 8 * q, :].bitcast(I32))
        tabs.append(load_table(2, late.tile([P, T], I32, name="tab2", align_bytes=64, offset=0)))
        w1raw.append(load_w1(1, late.tile([P, PASSES, 2 * BANK], U8, name="w1raw1", align_bytes=64, offset=4 * T)))
        for q in (0, 2, 1, 3):
            nc.sync.dma_start(moved2[32 * q : 32 * q + 4, :].bitcast(I32), staged[80 + 4 * q : 84 + 4 * q, :].bitcast(I32))
        planes = [moved[:, 0, :], moved[:, 1, :], moved2[:]]

        gains = keep.tile([P, GROUPS, PACK], F32, name="gains", tag="staged", align_bytes=64)
        nc.scalar.dma_start(gains[:], gain.rearrange("(b p i) -> p b i", p=P, i=PACK))

        got = {}
        w1c = {}

        def gather_words(a, pieces):
            width = S // pieces
            for c in range(pieces):
                words = keep.tile([P, width], U32, name=f"got{a}{c}", align_bytes=64)
                cols = slice(c * width // 16, (c + 1) * width // 16)
                nc.vector.tensor_copy(words[:], tabs[a][:].bitcast(U32).indirect(list1[:, cols]))
                for u in range(width // BANK):
                    got[a, c * width // BANK + u] = words[:, u * BANK : (u + 1) * BANK]

        def deal_words(a, b):
            dealt = keep.tile([P, 2 * BANK], U8, name=f"w1c{a}{b}", align_bytes=64)
            nc.scalar.copy(
                dealt[:].bitcast(U16).rearrange("p (i m) -> p i m", i=PACK),
                w1raw[b][:, a, :].bitcast(U16).rearrange("p (m i) -> p i m", i=PACK),
            )
            w1c[a, b] = dealt

        def first_product(bank, a, b, i, hf):
            cols = slice(hf * BANK, (hf + 1) * BANK)
            nc.tensor.matmul_mx(
                out=bank[:],
                lhsT=w1c[a, b][:, 2 * P * i : 2 * P * (i + 1)].bitcast(E2M1),
                lhsT_scale=planes[a][:, S + b * BANK + P * i : S + b * BANK + P * (i + 1)],
                rhs=got[a, hf].bitcast(E4M3),
                rhs_scale=planes[a][:, cols],
                start=(a == 0),
                stop=(a == PASSES - 1),
            )

        banks = {}
        for a in range(PASSES):
            deal_words(a, 0)
        for a in range(PASSES):
            gather_words(a, 1 if a == 1 else HALVES)
        for a in range(PASSES):
            deal_words(a, 1)

        def open_bank(b, i, hf):
            banks[b, i, hf] = psum.tile([P, BANK], F32, name=f"bank{b}{i}{hf}", tag="h", bufs=5)

        early = [(i, hf) for i in range(PACK) for hf in range(HALVES)][:5]
        for i, hf in early:
            open_bank(0, i, hf)
        for a in range(PASSES):
            for i, hf in early:
                first_product(banks[0, i, hf], a, 0, i, hf)
        waiting = [(b, i, hf) for b in range(GROUPS) for i in range(PACK) for hf in range(HALVES)][5:]

        w2raw = []
        for b in range(GROUPS):
            raw = wide.tile([P, PACK, N], F32, name=f"w2raw{b}", align_bytes=64, offset=4 * T * b)
            nc.sync.dma_start(raw[:], w2[b * 512 : (b + 1) * 512, :].rearrange("(p j) n -> p j n", j=PACK))
            w2raw.append(raw)

        w2h = [keep.tile([P, PACK * N], BF16, name=f"w2h{b}", align_bytes=64) for b in range(GROUPS)]

        def round_w2(copy, b, m0, width):
            dst = w2h[b][:].rearrange("p (t m j) -> p m t j", t=PACK, j=PACK)
            src = w2raw[b][:].rearrange("p j (m t) -> p m t j", t=PACK)
            copy(dst[:, m0 : m0 + width], src[:, m0 : m0 + width])

        def pool_copy(dst, src):
            nc.gpsimd.tensor_scalar(dst, src, 1.0, 0.0, ALU.mult, ALU.add)

        def quantize(name, src, width):
            codes = keep.tile([P, width], U32, name=name + "_codes", align_bytes=64)
            scales = keep.tile([P, width], U8, name=name + "_scales", align_bytes=64)
            nc.vector.quantize_mx(out=codes[:].bitcast(E4M3), scales=scales[:], in_=src)
            return codes, scales

        looked = [keep.tile([P, PACK, M], F32, name=f"looked{b}") for b in range(GROUPS)]

        def look(b, i, pieces, rows=None):
            h = keep.tile([P, S], F32, name=f"h{b}{i}", tag=f"h{b}{i}", align_bytes=64)
            tops = keep.tile([P, HALVES], F32, name=f"tops{b}{i}")
            for hf in range(HALVES):
                nc.vector.tensor_scalar(
                    h[:, hf * BANK : (hf + 1) * BANK], banks[b, i, hf][:], 1.0, None, ALU.mult, ALU.max,
                    accum_out=tops[:, hf : hf + 1],
                )
                if waiting:
                    place = waiting.pop(0)
                    open_bank(*place)
                    for a in range(PASSES):
                        first_product(banks[place], a, *place)
            neg_top = keep.tile([P, 1], F32, name=f"neg_top{b}{i}")
            nc.vector.tensor_reduce(neg_top[:], tops[:], mybir.AxisListType.X, ALU.max, negate=True)
            width = M // pieces
            for c in range(pieces):
                nc.scalar.activation(
                    out=looked[b][:, i, c * width : (c + 1) * width],
                    in_=h[:].indirect(list2[:, c * width // 16 : (c + 1) * width // 16]),
                    func=ACT.Exp,
                    bias=neg_top[:],
                )
                if rows is not None:
                    cols = slice(c * width, (c + 1) * width)
                    nc.scalar.activation(out=rows[:, i, cols], in_=looked[b][:, i, cols], func=ACT.Copy, scale=gains[:, b, i : i + 1])

        b0_rows = keep.tile([P, PACK, M], BF16, name="b0_rows", align_bytes=64)
        b1_rows = keep.tile([P, PACK, M], BF16, name="b1_rows", align_bytes=64)
        for c in range(4):
            round_w2(pool_copy, 0, 32 * c, 32)
        for i in range(PACK):
            look(0, i, 1)
            nc.gpsimd.tensor_scalar(b0_rows[:, i, :], looked[0][:, i, :], gains[:, 0, i : i + 1], 0.0, ALU.mult, ALU.add)
        round_w2(nc.vector.tensor_copy, 1, 0, 64)
        look(1, 0, 1, b1_rows)
        round_w2(nc.vector.tensor_copy, 1, 64, 64)
        w2q = [quantize("w2q0", w2h[0][:], N)]
        for i in range(1, PACK - 1):
            look(1, i, 1)
            nc.gpsimd.tensor_scalar(b1_rows[:, i, :], looked[1][:, i, :], gains[:, 1, i : i + 1], 0.0, ALU.mult, ALU.add)
        b0 = keep.tile([P, PACK * M], BF16, name="b0", align_bytes=64)
        for c in range(3):
            cols = slice(c * MQ, (c + 1) * MQ)
            nc.gpsimd.tensor_scalar(
                b0[:].rearrange("p (m i) -> p m i", i=PACK)[:, cols], b0_rows[:].rearrange("p i m -> p m i")[:, cols],
                1.0, 0.0, ALU.mult, ALU.add,
            )
        look(1, PACK - 1, 2, b1_rows)
        nc.vector.tensor_copy(
            b0[:, 3 * PACK * MQ :].rearrange("p (m i) -> p m i", i=PACK),
            b0_rows[:, :, 3 * MQ :].rearrange("p i m -> p m i"),
        )
        w2q.append(quantize("w2q1", w2h[1][:], N))
        b0q = quantize("b0q", b0[:], M)

        ybanks = [psum.tile([P, PACK, MQ], F32, name=f"ybank{c}", tag="y", bufs=3) for c in range(3)]
        ybanks.append(psum.tile([P, PACK, MQ], F32, name="ybank3", tag="h", bufs=5))

        def second_product(c, b, operand, m0):
            codes, scales = operand
            for t in range(PACK):
                nc.tensor.matmul_mx(
                    out=ybanks[c][:, t, :],
                    lhsT=w2q[b][0][:, P * t : P * (t + 1)].bitcast(E4M3),
                    lhsT_scale=w2q[b][1][:, P * t : P * (t + 1)],
                    rhs=codes[:, m0 : m0 + MQ].bitcast(E4M3),
                    rhs_scale=scales[:, m0 : m0 + MQ],
                    start=(b == 0 and t == 0),
                    stop=(b == GROUPS - 1 and t == PACK - 1),
                )

        for c in range(M // MQ):
            second_product(c, 0, b0q, c * MQ)

        y_codes = keep.tile([P, M], U32, name="y_codes", align_bytes=64)
        y_scales = keep.tile([P, M], U8, name="y_scales", align_bytes=64)
        out_rows = out_0.rearrange("(p t) m -> p t m", t=PACK)
        out_words = out_1[0].rearrange("p m t -> p (m t)").bitcast(I32)
        for c in range(M // MQ):
            b1 = keep.tile([P, PACK * MQ], BF16, name=f"b1{c}", align_bytes=64)
            nc.vector.tensor_copy(
                b1[:].rearrange("p (m i) -> p m i", i=PACK),
                b1_rows[:, :, c * MQ : (c + 1) * MQ].rearrange("p i m -> p m i"),
            )
            second_product(c, 1, quantize(f"b1q{c}", b1[:], MQ), 0)
        for c in range(M // MQ):
            cols = slice(c * MQ, (c + 1) * MQ)
            y = keep.tile([P, PACK, MQ], F32, name=f"y{c}")
            y_round = keep.tile([P, PACK * MQ], BF16, name=f"y_round{c}", align_bytes=64)
            if c == 3:
                nc.scalar.copy(y_round[:].rearrange("p (m t) -> p m t", t=PACK), ybanks[c][:].rearrange("p t m -> p m t"))
            nc.scalar.copy(y[:], ybanks[c][:])
            nc.sync.dma_start(out_rows[:, :, cols], y[:])
            if c < 3:
                nc.vector.tensor_copy(
                    y_round[:].rearrange("p (c e t) -> p c t e", e=4, t=PACK), y[:].rearrange("p t (c e) -> p c t e", e=4)
                )
            nc.vector.quantize_mx(out=y_codes[:, cols].bitcast(E4M3), scales=y_scales[:, cols], in_=y_round[:])
            if c % 2:
                pair = slice((c - 1) * MQ, (c + 1) * MQ)
                nc.sync.dma_start(out_words[:, pair], y_codes[:, pair].bitcast(I32))
        for q in range(QUADS):
            queue = nc.sync if q % 2 == 0 else nc.scalar
            queue.dma_start(out_2[0, 4 * q : 4 * q + 4, :].bitcast(I32), y_scales[32 * q : 32 * q + 4, :].bitcast(I32))
